import numpy as np
import ml_dtypes


def mxq(x, axis, fmt="e4m3"):
    dtype, down = {"e4m3": (ml_dtypes.float8_e4m3fn, 7), "e5m2": (ml_dtypes.float8_e5m2, 14)}[fmt]
    v = np.moveaxis(np.asarray(x, np.float32).astype(ml_dtypes.bfloat16).astype(np.float64), axis, -1)
    blocks = v.reshape(v.shape[:-1] + (-1, 32))
    amax = np.abs(blocks).max(-1, keepdims=True)
    byte = np.maximum(np.where(amax > 0, np.frexp(amax)[1] - 1 + 127, 0) - down, 1)
    scale = np.exp2(byte - 127.0)
    codes = (blocks / scale).astype(np.float32).astype(dtype).astype(np.float64)
    return np.moveaxis((codes * scale).reshape(v.shape), -1, axis)


WIDE = False


def mx_kscale(k):
    if not WIDE:
        return np.ones(k)
    levels = np.array([10, -10, 5, -5, 0])
    if k % 512:
        return np.exp2(np.random.permutation(np.resize(levels, k // 32))).repeat(32)
    a = np.empty((k // 512, 16))
    for p in range(k // 512):
        a[p, :8] = np.random.permutation(np.resize(levels, 8))
        for g in range(8):
            far = levels[np.abs(levels - a[p, g]) >= 10]
            a[p, g + 8] = far[np.random.randint(len(far))]
    return np.exp2(a.ravel()).repeat(32)


def f64(x):
    return np.asarray(x).astype(np.float64)


def striped(idx):
    return np.tile(idx.reshape(-1, 16).T, (8, 1)).astype(np.uint16)


def unstriped(offs):
    return offs[:16].T.reshape(-1).astype(np.int64)


def striped8(idx):
    return np.concatenate([x.reshape(-1, 16).T for x in idx]).astype(np.uint16)


def runs(offs, k):
    lists = np.stack([offs[16 * r : 16 * r + 16].T.reshape(-1) for r in range(8)]).astype(np.int64)
    return lists[np.arange(k) % 512 // 64]


def pack_weight(w):
    k, n = w.shape
    w = f64(np.asarray(w, np.float32).astype(ml_dtypes.bfloat16)).reshape(k // 32, 32, n)
    amax = np.abs(w).max(1)
    byte = np.clip(np.where(amax > 0, np.frexp(amax)[1] - 1 + 127 - 7, 1), 1, 254)
    scaled = (w * np.exp2(127.0 - byte)[:, None, :]).reshape(k, n).astype(np.float32)
    words = np.ascontiguousarray(scaled.reshape(k // 512, 128, 4, n).transpose(0, 1, 3, 2)).astype(ml_dtypes.float8_e4m3fn).view(np.uint8)
    return words, np.ascontiguousarray(byte.astype(np.uint8).reshape(k // 512, 16, n))


def unpack_weight(words, scales):
    g, p, n, _ = words.shape
    vals = np.ascontiguousarray(words).view(ml_dtypes.float8_e4m3fn).astype(np.float64) * np.repeat(np.exp2(scales.astype(np.float64) - 127.0), 8, axis=1)[..., None]
    return vals.transpose(0, 1, 3, 2).reshape(g * 512, n)

def planes(y):
    n, m = y.shape
    v = y.astype(np.float32).astype(ml_dtypes.bfloat16).astype(np.float64).reshape(n // 32, 32, m)
    top = np.abs(v).max(1)
    byte = np.clip(np.where(top > 0, np.frexp(top)[1] - 1 + 127 - 7, 1), 1, 254)
    codes = (v * np.exp2(127.0 - byte)[:, None, :]).reshape(n, m).astype(np.float32).astype(ml_dtypes.float8_e4m3fn).view(np.uint8)
    words = codes.reshape(n // 512, 128, 4, m).transpose(0, 1, 3, 2)
    return np.ascontiguousarray(words), np.ascontiguousarray(byte.astype(np.uint8).reshape(n // 512, 16, m))


K, T, S, H, C = 512, 2048, 512, 512, 512


def setup_inputs():
    n = np.random.standard_normal
    s = mx_kscale(K)[:, None]
    packed_xT = pack_weight(n((K, T)) * s)
    packed_w1 = pack_weight(n((K, H)) / np.sqrt(K) / s)
    return {
        "x_words": packed_xT[0],
        "x_scales": packed_xT[1],
        "w1_words": packed_w1[0],
        "w1_scales": packed_w1[1],
        "gs": (np.random.uniform(0.5, 1.5, (K, 1)) / s).astype(np.float32),
        "offs": striped(np.random.permutation(T)[:S]),
        "n1": striped8(np.stack([np.random.permutation(S) for _ in range(8)])),
        "cand": striped(np.random.permutation(T)[:C]),
        "n2": striped8(np.stack([np.random.permutation(S) for _ in range(8)])),
        "n3": striped8(np.stack([np.random.permutation(S) for _ in range(8)])),
    }


def reference(x_words, x_scales, w1_words, w1_scales, gs, offs, n1, cand, n2, n3):
    x_cand = unpack_weight(x_words, x_scales)[:, unstriped(cand)]
    xq = unpack_weight(x_words, x_scales)[:, unstriped(offs)]
    y = unpack_weight(w1_words, w1_scales).T @ xq
    st = y - (y[np.arange(H)[:, None], runs(n1, H)])
    z = f64(gs) * (st - (0.5 * (st[np.arange(H)[:, None], runs(n1, H)])))
    s = 0.0625 * ((x_cand.T @ mxq(z, 0, "e4m3")))
    pa = s[np.arange(C)[:, None], runs(n2, C)]
    pb = s[np.arange(C)[:, None], runs(n3, C)]
    out_0 = np.maximum(np.minimum(s, pa), np.minimum(np.maximum(s, pa), pb))
    return (out_0,) + planes(out_0)

@@ -1,0 +1,179 @@
+from contextlib import ExitStack
+
+import concourse.mybir as mybir
+
+K, T, S, H, C = 512, 2048, 512, 512, 512
+P = 128
+PACK = 4
+HALF = S // 2
+WIN = 2 * S
+
+FLOPS = 2 * K * H * S + 2 * H * C * S
+
+F32 = mybir.dt.float32
+BF16 = mybir.dt.bfloat16
+I32 = mybir.dt.int32
+U32 = mybir.dt.uint32
+U16 = mybir.dt.uint16
+U8 = mybir.dt.uint8
+FP8X4 = mybir.dt.float8_e4m3fn_x4
+ALU = mybir.AluOpType
+COPY = mybir.ActivationFunctionType.Copy
+
+
+def dealt(ap):
+    return ap.rearrange("p (t m) -> p m t", t=PACK)
+
+
+def as_listed(ap):
+    return ap.rearrange("p (m t) -> p m t", t=PACK)
+
+
+def tile_picked_candtwicemed_none_po_kernel(
+    tc, x_words, x_scales, w1_words, w1_scales, gs, offs, n1, cand, n2, n3, out_0, out_1, out_2
+):
+    nc = tc.nc
+    with ExitStack() as ctx:
+        sb = ctx.enter_context(tc.tile_pool(name="sb", bufs=1))
+        psum = ctx.enter_context(tc.psum_pool(name="psum", bufs=1))
+
+        offs_t = sb.tile([P, S // 16], U16, name="offs_t")
+        cand_t = sb.tile([P, C // 16], U16, name="cand_t")
+        n1_t = sb.tile([P, S // 16], U16, name="n1_t")
+        n2_t = sb.tile([P, S // 16], U16, name="n2_t")
+        n3_t = sb.tile([P, S // 16], U16, name="n3_t")
+        xw = sb.tile([P, T], U32, name="xw", align_bytes=64)
+        xs = sb.tile([P, T], U8, name="xs", align_bytes=64)
+        ww = sb.tile([P, H], U32, name="ww", align_bytes=64)
+        ws = sb.tile([P, H], U8, name="ws", align_bytes=64)
+        gs_t = sb.tile([P, PACK], F32, name="gs_t")
+
+        nc.vector.memset(xs[:].bitcast(I32), 0)
+        nc.vector.memset(ws[:].bitcast(I32), 0)
+        x_rows = x_words[0].rearrange("p n t -> p (n t)").bitcast(I32)
+        nc.sync.dma_start(offs_t[:], offs)
+        nc.sync.dma_start(xw[:, : T // 2].bitcast(I32), x_rows[:, : T // 2])
+        for q in range(4):
+            nc.sync.dma_start(xs[32 * q : 32 * q + 4, :].bitcast(I32), x_scales[0, 4 * q : 4 * q + 4, :].bitcast(I32))
+        nc.sync.dma_start(xw[:, T // 2 :].bitcast(I32), x_rows[:, T // 2 :])
+        nc.sync.dma_start(ww[:].bitcast(I32), w1_words[0].rearrange("p n t -> p (n t)").bitcast(I32))
+        for q in range(4):
+            nc.sync.dma_start(ws[32 * q : 32 * q + 4, :].bitcast(I32), w1_scales[0, 4 * q : 4 * q + 4, :].bitcast(I32))
+        nc.sync.dma_start(gs_t[:], gs.rearrange("(p t) o -> p (t o)", t=PACK))
+        nc.sync.dma_start(n1_t[:], n1)
+        nc.sync.dma_start(cand_t[:], cand)
+        nc.sync.dma_start(n2_t[:], n2)
+        nc.sync.dma_start(n3_t[:], n3)
+
+        win_a = [sb.tile([P, WIN], F32, name=f"win_a{t}", align_bytes=64) for t in range(PACK)]
+        win_b = [sb.tile([P, WIN], F32, name=f"win_b{t}", align_bytes=64) for t in range(PACK)]
+        for t in range(PACK):
+            nc.vector.memset(win_a[t][:, S:], 0.0)
+
+        xq_w = sb.tile([P, S], U32, name="xq_w", align_bytes=64)
+        xq_s = sb.tile([P, S], U8, name="xq_s", align_bytes=64)
+        xc_w = sb.tile([P, C], U32, name="xc_w", align_bytes=64)
+        xc_s0 = sb.tile([P, C], U8, name="xc_s0", align_bytes=64)
+        xc_s = sb.tile([P, C], U8, name="xc_s", align_bytes=64)
+        w_w = sb.tile([P, H], U32, name="w_w", align_bytes=64)
+        w_s = sb.tile([P, H], U8, name="w_s", align_bytes=64)
+
+        nc.vector.tensor_copy(xq_s[:], xs[:].indirect(offs_t[:]))
+        nc.vector.tensor_copy(xq_w[:], xw[:].indirect(offs_t[:]))
+        nc.vector.tensor_copy(dealt(w_w[:]), as_listed(ww[:]))
+        nc.vector.tensor_copy(dealt(w_s[:]), as_listed(ws[:]))
+        nc.vector.tensor_copy(xc_s0[:], xs[:].indirect(cand_t[:]))
+        nc.vector.tensor_copy(dealt(xc_w[:]), xw[:].indirect(cand_t[:]))
+        nc.vector.tensor_copy(dealt(xc_s[:]), as_listed(xc_s0[:]))
+
+        y_ps = [psum.tile([P, S], F32, name=f"y_ps{t}") for t in range(PACK)]
+        s_ps = [psum.tile([P, S], F32, name=f"s_ps{t}") for t in range(PACK)]
+        nst = [sb.tile([P, S], F32, name=f"nst{t}", align_bytes=64) for t in range(PACK)]
+        z = sb.tile([P, PACK, S], F32, name="z", align_bytes=64)
+        zi = sb.tile([P, S, PACK], BF16, name="zi", align_bytes=64)
+        zq_w = sb.tile([P, S], U32, name="zq_w", align_bytes=64)
+        zq_s = sb.tile([P, S], U8, name="zq_s", align_bytes=64)
+
+        for t in range(PACK):
+            cols = slice(t * P, (t + 1) * P)
+            nc.tensor.matmul_mx(
+                out=y_ps[t][:], lhsT=w_w[:, cols].bitcast(FP8X4), lhsT_scale=w_s[:, cols],
+                rhs=xq_w[:].bitcast(FP8X4), rhs_scale=xq_s[:], start=True, stop=True,
+            )
+            nc.scalar.activation(win_a[t][:, :S], y_ps[t][:], COPY, scale=gs_t[:, t : t + 1])
+            nc.scalar.activation(win_b[t][:, S:], y_ps[t][:], COPY, scale=gs_t[:, t : t + 1])
+        for t in range(PACK):
+            nc.vector.tensor_tensor(nst[t][:], win_a[t][:].indirect(n1_t[:]), win_b[t][:, S:], ALU.subtract)
+            nc.scalar.activation(win_b[t][:, :S], nst[t][:], COPY, scale=0.5)
+
+        halves = [slice(0, HALF), slice(HALF, S)]
+        list_halves = [slice(0, HALF // 16), slice(HALF // 16, S // 16)]
+
+        def weave(dst, src, pair, cols, on_scalar):
+            rows = slice(2 * pair, 2 * pair + 2)
+            out_ap = dst[:, cols, rows]
+            in_ap = src[:, rows, cols].rearrange("p t n -> p n t")
+            if on_scalar:
+                nc.scalar.copy(out_ap, in_ap)
+            else:
+                nc.vector.tensor_copy(out_ap, in_ap)
+
+        def quantise(words, scales, src, cols):
+            nc.vector.quantize_mx(
+                out=words[:, cols].bitcast(FP8X4), scales=scales[:, cols],
+                in_=src[:, cols, :].rearrange("p n t -> p (n t)"),
+            )
+
+        for t in range(2):
+            nc.vector.tensor_tensor(z[:, t, :], win_b[t][:].indirect(n1_t[:]), nst[t][:], ALU.subtract)
+        weave(zi, z, 0, slice(0, S), True)
+        for h in range(2):
+            for t in range(2, PACK):
+                nc.vector.tensor_tensor(
+                    z[:, t, halves[h]], win_b[t][:].indirect(n1_t[:, list_halves[h]]), nst[t][:, halves[h]], ALU.subtract
+                )
+            weave(zi, z, 1, halves[h], h == 0)
+        for h in range(2):
+            quantise(zq_w, zq_s, zi, halves[h])
+
+        s_copy = [sb.tile([P, S], F32, name=f"s_copy{t}", align_bytes=64) for t in range(PACK)]
+        for t in range(PACK):
+            cols = slice(t * P, (t + 1) * P)
+            nc.tensor.matmul_mx(
+                out=s_ps[t][:], lhsT=xc_w[:, cols].bitcast(FP8X4), lhsT_scale=xc_s[:, cols],
+                rhs=zq_w[:].bitcast(FP8X4), rhs_scale=zq_s[:], start=True, stop=True,
+            )
+            nc.scalar.activation(win_a[t][:, :S], s_ps[t][:], COPY, scale=0.0625)
+            nc.scalar.activation(s_copy[t][:], s_ps[t][:], COPY, scale=0.0625)
+
+        res = sb.tile([P, PACK, S], F32, name="res", align_bytes=64)
+        ri = sb.tile([P, S, PACK], BF16, name="ri", align_bytes=64)
+        rq_w = sb.tile([P, S], U32, name="rq_w", align_bytes=64)
+        rq_s = sb.tile([P, S], U8, name="rq_s", align_bytes=64)
+        da = [sb.tile([P, S], F32, name=f"da{t}", align_bytes=64) for t in range(PACK)]
+        db = [sb.tile([P, S], F32, name=f"db{t}", align_bytes=64) for t in range(PACK)]
+        up = [sb.tile([P, S], F32, name=f"up{t}", align_bytes=64) for t in range(PACK)]
+        out_rows = out_0.rearrange("(p t) n -> p t n", t=PACK)
+
+        def median(t, cols):
+            nc.vector.scalar_tensor_tensor(up[t][:, cols], da[t][:, cols], 0.0, db[t][:, cols], ALU.max, ALU.min)
+            nc.vector.scalar_tensor_tensor(db[t][:, cols], da[t][:, cols], 0.0, up[t][:, cols], ALU.min, ALU.max)
+            nc.vector.tensor_tensor(res[:, t, cols], db[t][:, cols], s_copy[t][:, cols], ALU.add)
+            nc.sync.dma_start(out_rows[:, t, cols], res[:, t, cols])
+
+        for t in range(PACK):
+            nc.vector.tensor_tensor(da[t][:], win_a[t][:].indirect(n2_t[:]), s_copy[t][:], ALU.subtract)
+            nc.vector.tensor_tensor(db[t][:], win_a[t][:].indirect(n3_t[:]), s_copy[t][:], ALU.subtract)
+            if t < PACK - 1:
+                median(t, slice(0, S))
+            if t == 1:
+                weave(ri, res, 0, slice(0, S), True)
+        words_out = out_1[0].rearrange("p n t -> p (n t)").bitcast(I32)
+        for h in range(2):
+            median(PACK - 1, halves[h])
+            weave(ri, res, 1, halves[h], h == 0)
+        for h in range(2):
+            quantise(rq_w, rq_s, ri, halves[h])
+            nc.sync.dma_start(words_out[:, halves[h]], rq_w[:, halves[h]].bitcast(I32))
+        for q in range(4):
+            nc.scalar.dma_start(out_2[0, 4 * q : 4 * q + 4, :].bitcast(I32), rq_s[32 * q : 32 * q + 4, :].bitcast(I32))

@@ -1,6 +1,7 @@
 from contextlib import ExitStack
 
 import concourse.mybir as mybir
+from concourse.masks import make_identity
 
 K, T, S, H, C = 512, 2048, 512, 512, 512
 P = 128
@@ -19,6 +20,7 @@ U8 = mybir.dt.uint8
 FP8X4 = mybir.dt.float8_e4m3fn_x4
 ALU = mybir.AluOpType
 COPY = mybir.ActivationFunctionType.Copy
+RELU = mybir.ActivationFunctionType.Relu
 
 
 def dealt(ap):
@@ -65,6 +67,9 @@ def tile_picked_candtwicemed_none_po_kernel(
         nc.sync.dma_start(n2_t[:], n2)
         nc.sync.dma_start(n3_t[:], n3)
 
+        ident = sb.tile([P, P], F32, name="ident", align_bytes=64)
+        make_identity(nc, ident[:])
+
         win_a = [sb.tile([P, WIN], F32, name=f"win_a{t}", align_bytes=64) for t in range(PACK)]
         win_b = [sb.tile([P, WIN], F32, name=f"win_b{t}", align_bytes=64) for t in range(PACK)]
         for t in range(PACK):
@@ -109,8 +114,7 @@ def tile_picked_candtwicemed_none_po_kernel(
         halves = [slice(0, HALF), slice(HALF, S)]
         list_halves = [slice(0, HALF // 16), slice(HALF // 16, S // 16)]
 
-        def weave(dst, src, pair, cols, on_scalar):
-            rows = slice(2 * pair, 2 * pair + 2)
+        def weave(dst, src, rows, cols, on_scalar):
             out_ap = dst[:, cols, rows]
             in_ap = src[:, rows, cols].rearrange("p t n -> p n t")
             if on_scalar:
@@ -124,27 +128,37 @@ def tile_picked_candtwicemed_none_po_kernel(
                 in_=src[:, cols, :].rearrange("p n t -> p (n t)"),
             )
 
-        for t in range(2):
+        whole = slice(0, S)
+        last = PACK - 1
+        for t in range(last):
             nc.vector.tensor_tensor(z[:, t, :], win_b[t][:].indirect(n1_t[:]), nst[t][:], ALU.subtract)
-        weave(zi, z, 0, slice(0, S), True)
+            if t == 1:
+                weave(zi, z, slice(0, 2), whole, True)
         for h in range(2):
-            for t in range(2, PACK):
-                nc.vector.tensor_tensor(
-                    z[:, t, halves[h]], win_b[t][:].indirect(n1_t[:, list_halves[h]]), nst[t][:, halves[h]], ALU.subtract
-                )
-            weave(zi, z, 1, halves[h], h == 0)
+            nc.vector.tensor_tensor(
+                z[:, last, halves[h]], win_b[last][:].indirect(n1_t[:, list_halves[h]]), nst[last][:, halves[h]], ALU.subtract
+            )
+            weave(zi, z, slice(2, 4), halves[h], h == 0)
         for h in range(2):
             quantise(zq_w, zq_s, zi, halves[h])
 
-        s_copy = [sb.tile([P, S], F32, name=f"s_copy{t}", align_bytes=64) for t in range(PACK)]
-        for t in range(PACK):
-            cols = slice(t * P, (t + 1) * P)
+        neg_s = [sb.tile([P, S], F32, name=f"neg_s{t}", align_bytes=64) for t in range(PACK)]
+
+        def scores(t, bank, cols):
+            rows = slice(t * P, (t + 1) * P)
             nc.tensor.matmul_mx(
-                out=s_ps[t][:], lhsT=xc_w[:, cols].bitcast(FP8X4), lhsT_scale=xc_s[:, cols],
-                rhs=zq_w[:].bitcast(FP8X4), rhs_scale=zq_s[:], start=True, stop=True,
+                out=bank[:, cols], lhsT=xc_w[:, rows].bitcast(FP8X4), lhsT_scale=xc_s[:, rows],
+                rhs=zq_w[:, cols].bitcast(FP8X4), rhs_scale=zq_s[:, cols], start=True, stop=True,
             )
-            nc.scalar.activation(win_a[t][:, :S], s_ps[t][:], COPY, scale=0.0625)
-            nc.scalar.activation(s_copy[t][:], s_ps[t][:], COPY, scale=0.0625)
+            nc.scalar.activation(win_a[t][:, cols], bank[:, cols], COPY, scale=0.0625)
+
+        scores(0, s_ps[0], halves[0])
+        scores(0, y_ps[0], halves[1])
+        nc.vector.tensor_scalar(neg_s[0][:, halves[0]], s_ps[0][:, halves[0]], -0.0625, None, ALU.mult)
+        nc.scalar.activation(neg_s[0][:, halves[1]], y_ps[0][:, halves[1]], COPY, scale=-0.0625)
+        for t in range(1, PACK):
+            scores(t, s_ps[t], whole)
+            nc.scalar.activation(neg_s[t][:], s_ps[t][:], COPY, scale=-0.0625)
 
         res = sb.tile([P, PACK, S], F32, name="res", align_bytes=64)
         ri = sb.tile([P, S, PACK], BF16, name="ri", align_bytes=64)
@@ -153,27 +167,78 @@ def tile_picked_candtwicemed_none_po_kernel(
         da = [sb.tile([P, S], F32, name=f"da{t}", align_bytes=64) for t in range(PACK)]
         db = [sb.tile([P, S], F32, name=f"db{t}", align_bytes=64) for t in range(PACK)]
         up = [sb.tile([P, S], F32, name=f"up{t}", align_bytes=64) for t in range(PACK)]
+        below = sb.tile([P, S], F32, name="below", align_bytes=64)
+        low_t = sb.tile([P, S], F32, name="low_t", align_bytes=64)
+        rise_t = sb.tile([P, S], F32, name="rise_t", align_bytes=64)
+        sum_t = sb.tile([P, S], F32, name="sum_t", align_bytes=64)
         out_rows = out_0.rearrange("(p t) n -> p t n", t=PACK)
 
-        def median(t, cols):
+        def turned_sum(bank, terms):
+            for b in range(S // P):
+                blk = slice(b * P, (b + 1) * P)
+                for i, term in enumerate(terms):
+                    nc.tensor.matmul(
+                        bank[:, blk], term[:, blk], ident[:], start=i == 0, stop=i == len(terms) - 1, is_transpose=True
+                    )
+
+        def fetch(dst, t, lst, cols, list_cols):
+            nc.vector.tensor_tensor(dst[t][:, cols], win_a[t][:].indirect(lst[:, list_cols]), neg_s[t][:, cols], ALU.add)
+
+        def cap(t, cols):
             nc.vector.scalar_tensor_tensor(up[t][:, cols], da[t][:, cols], 0.0, db[t][:, cols], ALU.max, ALU.min)
+
+        def floor(t, cols):
             nc.vector.scalar_tensor_tensor(db[t][:, cols], da[t][:, cols], 0.0, up[t][:, cols], ALU.min, ALU.max)
-            nc.vector.tensor_tensor(res[:, t, cols], db[t][:, cols], s_copy[t][:, cols], ALU.add)
+
+        def finish(t, cols):
+            nc.vector.tensor_tensor(res[:, t, cols], db[t][:, cols], neg_s[t][:, cols], ALU.subtract)
             nc.sync.dma_start(out_rows[:, t, cols], res[:, t, cols])
 
-        for t in range(PACK):
-            nc.vector.tensor_tensor(da[t][:], win_a[t][:].indirect(n2_t[:]), s_copy[t][:], ALU.subtract)
-            nc.vector.tensor_tensor(db[t][:], win_a[t][:].indirect(n3_t[:]), s_copy[t][:], ALU.subtract)
-            if t < PACK - 1:
-                median(t, slice(0, S))
-            if t == 1:
-                weave(ri, res, 0, slice(0, S), True)
-        words_out = out_1[0].rearrange("p n t -> p (n t)").bitcast(I32)
+        def store_from(bank, t):
+            nc.scalar.copy(res[:, t, :], bank[:])
+            nc.sync.dma_start(out_rows[:, t, :], res[:, t, :])
+
+        all16 = slice(0, S // 16)
         for h in range(2):
-            median(PACK - 1, halves[h])
-            weave(ri, res, 1, halves[h], h == 0)
+            fetch(da, 0, n2_t, halves[h], list_halves[h])
+        nc.scalar.activation(below[:], da[0][:], RELU, scale=-1.0)
+        turned_sum(y_ps[1], [below, neg_s[0]])
+        nc.scalar.activation(low_t[:], y_ps[1][:], COPY, scale=-1.0)
+        fetch(db, 0, n3_t, whole, all16)
+        fetch(da, 1, n2_t, whole, all16)
+        cap(0, whole)
+        turned_sum(y_ps[2], [up[0], below])
+        nc.scalar.activation(rise_t[:], y_ps[2][:], RELU)
+        turned_sum(s_ps[0], [low_t, rise_t])
+        store_from(s_ps[0], 0)
+        weave(ri, res, slice(0, 1), halves[0], True)
+        fetch(db, 1, n3_t, whole, all16)
+        cap(1, whole)
+        fetch(da, 2, n2_t, whole, all16)
+        floor(1, whole)
+        turned_sum(y_ps[3], [win_a[1], db[1]])
+        nc.scalar.copy(sum_t[:], y_ps[3][:])
+        turned_sum(s_ps[1], [sum_t])
+        store_from(s_ps[1], 1)
+        weave(ri, res, slice(0, 2), halves[1], True)
+        fetch(db, 2, n3_t, whole, all16)
+        fetch(da, 3, n2_t, whole, all16)
+        cap(2, whole)
+        fetch(db, 3, n3_t, whole, all16)
+        floor(2, whole)
+        cap(3, halves[0])
+        finish(2, whole)
+        cap(3, halves[1])
+        floor(3, halves[0])
+        floor(3, halves[1])
+        words_out = out_1[0].rearrange("p n t -> p (n t)").bitcast(I32)
+        finish(3, halves[0])
+        weave(ri, res, slice(1, 4), halves[0], True)
+        finish(3, halves[1])
+        weave(ri, res, slice(2, 4), halves[1], False)
         for h in range(2):
             quantise(rq_w, rq_s, ri, halves[h])
             nc.sync.dma_start(words_out[:, halves[h]], rq_w[:, halves[h]].bitcast(I32))
         for q in range(4):
-            nc.scalar.dma_start(out_2[0, 4 * q : 4 * q + 4, :].bitcast(I32), rq_s[32 * q : 32 * q + 4, :].bitcast(I32))
+            queue = nc.scalar if q < 2 else nc.sync
+            queue.dma_start(out_2[0, 4 * q : 4 * q + 4, :].bitcast(I32), rq_s[32 * q : 32 * q + 4, :].bitcast(I32))

@@ -213,8 +213,9 @@ def tile_picked_candtwicemed_none_po_kernel(
         store_from(s_ps[0], 0)
         weave(ri, res, slice(0, 1), halves[0], True)
         fetch(db, 1, n3_t, whole, all16)
+        fetch(da, 2, n2_t, halves[0], list_halves[0])
         cap(1, whole)
-        fetch(da, 2, n2_t, whole, all16)
+        fetch(da, 2, n2_t, halves[1], list_halves[1])
         floor(1, whole)
         turned_sum(y_ps[3], [win_a[1], db[1]])
         nc.scalar.copy(sum_t[:], y_ps[3][:])

@@ -61,25 +61,25 @@ def tile_picked_candtwicemed_none_po_kernel(
         nc.sync.dma_start(ww[:].bitcast(I32), w1_words[0].rearrange("p n t -> p (n t)").bitcast(I32))
         for q in range(4):
             nc.sync.dma_start(ws[32 * q : 32 * q + 4, :].bitcast(I32), w1_scales[0, 4 * q : 4 * q + 4, :].bitcast(I32))
+        nc.sync.dma_start(cand_t[:], cand)
         nc.sync.dma_start(gs_t[:], gs.rearrange("(p t) o -> p (t o)", t=PACK))
         nc.sync.dma_start(n1_t[:], n1)
-        nc.sync.dma_start(cand_t[:], cand)
         nc.sync.dma_start(n2_t[:], n2)
         nc.sync.dma_start(n3_t[:], n3)
 
-        ident = sb.tile([P, P], F32, name="ident", align_bytes=64)
-        make_identity(nc, ident[:])
 
         win_a = [sb.tile([P, WIN], F32, name=f"win_a{t}", align_bytes=64) for t in range(PACK)]
         win_b = [sb.tile([P, WIN], F32, name=f"win_b{t}", align_bytes=64) for t in range(PACK)]
         for t in range(PACK):
             nc.vector.memset(win_a[t][:, S:], 0.0)
+        ident = sb.tile([P, P], F32, name="ident", align_bytes=64)
+        nc.vector.memset(ident[:], 0.0)
+        make_identity(nc, ident[:], nomemset=True)
 
         xq_w = sb.tile([P, S], U32, name="xq_w", align_bytes=64)
         xq_s = sb.tile([P, S], U8, name="xq_s", align_bytes=64)
         xc_w = sb.tile([P, C], U32, name="xc_w", align_bytes=64)
         xc_s0 = sb.tile([P, C], U8, name="xc_s0", align_bytes=64)
-        xc_s = sb.tile([P, C], U8, name="xc_s", align_bytes=64)
         w_w = sb.tile([P, H], U32, name="w_w", align_bytes=64)
         w_s = sb.tile([P, H], U8, name="w_s", align_bytes=64)
 
@@ -89,15 +89,16 @@ def tile_picked_candtwicemed_none_po_kernel(
         nc.vector.tensor_copy(dealt(w_s[:]), as_listed(ws[:]))
         nc.vector.tensor_copy(xc_s0[:], xs[:].indirect(cand_t[:]))
         nc.vector.tensor_copy(dealt(xc_w[:]), xw[:].indirect(cand_t[:]))
-        nc.vector.tensor_copy(dealt(xc_s[:]), as_listed(xc_s0[:]))
 
+        xc_s_first = sb.tile([P, P], U8, name="xc_s_first", align_bytes=64)
+        nc.vector.tensor_copy(xc_s_first[:], as_listed(xc_s0[:])[:, :, 0])
         y_ps = [psum.tile([P, S], F32, name=f"y_ps{t}") for t in range(PACK)]
         s_ps = [psum.tile([P, S], F32, name=f"s_ps{t}") for t in range(PACK)]
         nst = [sb.tile([P, S], F32, name=f"nst{t}", align_bytes=64) for t in range(PACK)]
         z = sb.tile([P, PACK, S], F32, name="z", align_bytes=64)
-        zi = sb.tile([P, S, PACK], BF16, name="zi", align_bytes=64)
-        zq_w = sb.tile([P, S], U32, name="zq_w", align_bytes=64)
-        zq_s = sb.tile([P, S], U8, name="zq_s", align_bytes=64)
+        zi = sb.tile([P, S, PACK], BF16, name="zi", tag="zi", align_bytes=64)
+        zq_w = [sb.tile([P, HALF], U32, name=f"zq_w{h}", align_bytes=64) for h in range(2)]
+        zq_s = [sb.tile([P, HALF], U8, name=f"zq_s{h}", align_bytes=64) for h in range(2)]
 
         for t in range(PACK):
             cols = slice(t * P, (t + 1) * P)
@@ -124,7 +125,7 @@ def tile_picked_candtwicemed_none_po_kernel(
 
         def quantise(words, scales, src, cols):
             nc.vector.quantize_mx(
-                out=words[:, cols].bitcast(FP8X4), scales=scales[:, cols],
+                out=words.bitcast(FP8X4), scales=scales,
                 in_=src[:, cols, :].rearrange("p n t -> p (n t)"),
             )
 
@@ -139,25 +140,29 @@ def tile_picked_candtwicemed_none_po_kernel(
                 z[:, last, halves[h]], win_b[last][:].indirect(n1_t[:, list_halves[h]]), nst[last][:, halves[h]], ALU.subtract
             )
             weave(zi, z, slice(2, 4), halves[h], h == 0)
-        for h in range(2):
-            quantise(zq_w, zq_s, zi, halves[h])
+        for h in (1, 0):
+            quantise(zq_w[h][:], zq_s[h][:], zi, halves[h])
+        xc_s_rest = sb.tile([P, last * P], U8, name="xc_s_rest", tag="zi", align_bytes=64)
+        nc.vector.tensor_copy(xc_s_rest[:].rearrange("p (t m) -> p m t", t=last), as_listed(xc_s0[:])[:, :, 1:])
+        xc_s = [xc_s_first[:]] + [xc_s_rest[:, t * P : (t + 1) * P] for t in range(last)]
 
         neg_s = [sb.tile([P, S], F32, name=f"neg_s{t}", align_bytes=64) for t in range(PACK)]
 
-        def scores(t, bank, cols):
-            rows = slice(t * P, (t + 1) * P)
+        def scores(t, bank, h):
             nc.tensor.matmul_mx(
-                out=bank[:, cols], lhsT=xc_w[:, rows].bitcast(FP8X4), lhsT_scale=xc_s[:, rows],
-                rhs=zq_w[:, cols].bitcast(FP8X4), rhs_scale=zq_s[:, cols], start=True, stop=True,
+                out=bank[:, halves[h]], lhsT=xc_w[:, t * P : (t + 1) * P].bitcast(FP8X4), lhsT_scale=xc_s[t],
+                rhs=zq_w[h][:].bitcast(FP8X4), rhs_scale=zq_s[h][:], start=True, stop=True,
             )
-            nc.scalar.activation(win_a[t][:, cols], bank[:, cols], COPY, scale=0.0625)
 
-        scores(0, s_ps[0], halves[0])
-        scores(0, y_ps[0], halves[1])
-        nc.vector.tensor_scalar(neg_s[0][:, halves[0]], s_ps[0][:, halves[0]], -0.0625, None, ALU.mult)
-        nc.scalar.activation(neg_s[0][:, halves[1]], y_ps[0][:, halves[1]], COPY, scale=-0.0625)
+        for h, bank in ((1, y_ps[0]), (0, s_ps[0])):
+            scores(0, bank, h)
+            nc.scalar.activation(win_a[0][:, halves[h]], bank[:, halves[h]], COPY, scale=0.0625)
+        nc.vector.tensor_scalar(neg_s[0][:, halves[1]], y_ps[0][:, halves[1]], -0.0625, None, ALU.mult)
+        nc.scalar.activation(neg_s[0][:, halves[0]], s_ps[0][:, halves[0]], COPY, scale=-0.0625)
         for t in range(1, PACK):
-            scores(t, s_ps[t], whole)
+            for h in range(2):
+                scores(t, s_ps[t], h)
+            nc.scalar.activation(win_a[t][:, :S], s_ps[t][:], COPY, scale=0.0625)
             nc.scalar.activation(neg_s[t][:], s_ps[t][:], COPY, scale=-0.0625)
 
         res = sb.tile([P, PACK, S], F32, name="res", align_bytes=64)
@@ -192,14 +197,13 @@ def tile_picked_candtwicemed_none_po_kernel(
 
         def finish(t, cols):
             nc.vector.tensor_tensor(res[:, t, cols], db[t][:, cols], neg_s[t][:, cols], ALU.subtract)
-            nc.sync.dma_start(out_rows[:, t, cols], res[:, t, cols])
 
         def store_from(bank, t):
             nc.scalar.copy(res[:, t, :], bank[:])
             nc.sync.dma_start(out_rows[:, t, :], res[:, t, :])
 
         all16 = slice(0, S // 16)
-        for h in range(2):
+        for h in (1, 0):
             fetch(da, 0, n2_t, halves[h], list_halves[h])
         nc.scalar.activation(below[:], da[0][:], RELU, scale=-1.0)
         turned_sum(y_ps[1], [below, neg_s[0]])
@@ -229,6 +233,7 @@ def tile_picked_candtwicemed_none_po_kernel(
         floor(2, whole)
         cap(3, halves[0])
         finish(2, whole)
+        nc.sync.dma_start(out_rows[:, 2, :], res[:, 2, :])
         cap(3, halves[1])
         floor(3, halves[0])
         floor(3, halves[1])
@@ -236,9 +241,10 @@ def tile_picked_candtwicemed_none_po_kernel(
         finish(3, halves[0])
         weave(ri, res, slice(1, 4), halves[0], True)
         finish(3, halves[1])
+        nc.sync.dma_start(out_rows[:, 3, :], res[:, 3, :])
         weave(ri, res, slice(2, 4), halves[1], False)
         for h in range(2):
-            quantise(rq_w, rq_s, ri, halves[h])
+            quantise(rq_w[:, halves[h]], rq_s[:, halves[h]], ri, halves[h])
             nc.sync.dma_start(words_out[:, halves[h]], rq_w[:, halves[h]].bitcast(I32))
         for q in range(4):
             queue = nc.scalar if q < 2 else nc.sync

@@ -73,8 +73,7 @@ def tile_picked_candtwicemed_none_po_kernel(
         for t in range(PACK):
             nc.vector.memset(win_a[t][:, S:], 0.0)
         ident = sb.tile([P, P], F32, name="ident", align_bytes=64)
-        nc.vector.memset(ident[:], 0.0)
-        make_identity(nc, ident[:], nomemset=True)
+        make_identity(nc, ident[:])
 
         xq_w = sb.tile([P, S], U32, name="xq_w", align_bytes=64)
         xq_s = sb.tile([P, S], U8, name="xq_s", align_bytes=64)
@@ -197,6 +196,7 @@ def tile_picked_candtwicemed_none_po_kernel(
 
         def finish(t, cols):
             nc.vector.tensor_tensor(res[:, t, cols], db[t][:, cols], neg_s[t][:, cols], ALU.subtract)
+            nc.sync.dma_start(out_rows[:, t, cols], res[:, t, cols])
 
         def store_from(bank, t):
             nc.scalar.copy(res[:, t, :], bank[:])
@@ -233,7 +233,6 @@ def tile_picked_candtwicemed_none_po_kernel(
         floor(2, whole)
         cap(3, halves[0])
         finish(2, whole)
-        nc.sync.dma_start(out_rows[:, 2, :], res[:, 2, :])
         cap(3, halves[1])
         floor(3, halves[0])
         floor(3, halves[1])
@@ -241,7 +240,6 @@ def tile_picked_candtwicemed_none_po_kernel(
         finish(3, halves[0])
         weave(ri, res, slice(1, 4), halves[0], True)
         finish(3, halves[1])
-        nc.sync.dma_start(out_rows[:, 3, :], res[:, 3, :])
         weave(ri, res, slice(2, 4), halves[1], False)
         for h in range(2):
             quantise(rq_w[:, halves[h]], rq_s[:, halves[h]], ri, halves[h])

from contextlib import ExitStack

import concourse.mybir as mybir
from concourse.masks import make_identity

K, T, S, H, C = 512, 2048, 512, 512, 512
P = 128
PACK = 4
HALF = S // 2
WIN = 2 * S

FLOPS = 2 * K * H * S + 2 * H * C * S

F32 = mybir.dt.float32
BF16 = mybir.dt.bfloat16
I32 = mybir.dt.int32
U32 = mybir.dt.uint32
U16 = mybir.dt.uint16
U8 = mybir.dt.uint8
FP8X4 = mybir.dt.float8_e4m3fn_x4
ALU = mybir.AluOpType
COPY = mybir.ActivationFunctionType.Copy
RELU = mybir.ActivationFunctionType.Relu


def dealt(ap):
    return ap.rearrange("p (t m) -> p m t", t=PACK)


def as_listed(ap):
    return ap.rearrange("p (m t) -> p m t", t=PACK)


def tile_picked_candtwicemed_none_po_kernel(
    tc, x_words, x_scales, w1_words, w1_scales, gs, offs, n1, cand, n2, n3, out_0, out_1, out_2
):
    nc = tc.nc
    with ExitStack() as ctx:
        sb = ctx.enter_context(tc.tile_pool(name="sb", bufs=1))
        psum = ctx.enter_context(tc.psum_pool(name="psum", bufs=1))

        offs_t = sb.tile([P, S // 16], U16, name="offs_t")
        cand_t = sb.tile([P, C // 16], U16, name="cand_t")
        n1_t = sb.tile([P, S // 16], U16, name="n1_t")
        n2_t = sb.tile([P, S // 16], U16, name="n2_t")
        n3_t = sb.tile([P, S // 16], U16, name="n3_t")
        xw = sb.tile([P, T], U32, name="xw", align_bytes=64)
        xs = sb.tile([P, T], U8, name="xs", align_bytes=64)
        ww = sb.tile([P, H], U32, name="ww", align_bytes=64)
        ws = sb.tile([P, H], U8, name="ws", align_bytes=64)
        gs_t = sb.tile([P, PACK], F32, name="gs_t")

        nc.vector.memset(xs[:].bitcast(I32), 0)
        nc.vector.memset(ws[:].bitcast(I32), 0)
        x_rows = x_words[0].rearrange("p n t -> p (n t)").bitcast(I32)
        nc.sync.dma_start(offs_t[:], offs)
        nc.sync.dma_start(xw[:, : T // 2].bitcast(I32), x_rows[:, : T // 2])
        for q in range(4):
            nc.sync.dma_start(xs[32 * q : 32 * q + 4, :].bitcast(I32), x_scales[0, 4 * q : 4 * q + 4, :].bitcast(I32))
        nc.sync.dma_start(xw[:, T // 2 :].bitcast(I32), x_rows[:, T // 2 :])
        nc.sync.dma_start(ww[:].bitcast(I32), w1_words[0].rearrange("p n t -> p (n t)").bitcast(I32))
        for q in range(4):
            nc.sync.dma_start(ws[32 * q : 32 * q + 4, :].bitcast(I32), w1_scales[0, 4 * q : 4 * q + 4, :].bitcast(I32))
        nc.sync.dma_start(cand_t[:], cand)
        nc.sync.dma_start(gs_t[:], gs.rearrange("(p t) o -> p (t o)", t=PACK))
        nc.sync.dma_start(n1_t[:], n1)
        nc.sync.dma_start(n2_t[:], n2)
        nc.sync.dma_start(n3_t[:], n3)


        win_a = [sb.tile([P, WIN], F32, name=f"win_a{t}", align_bytes=64) for t in range(PACK)]
        win_b = [sb.tile([P, WIN], F32, name=f"win_b{t}", align_bytes=64) for t in range(PACK)]
        for t in range(PACK):
            nc.vector.memset(win_a[t][:, S:], 0.0)
        ident = sb.tile([P, P], F32, name="ident", align_bytes=64)
        make_identity(nc, ident[:])

        xq_w = sb.tile([P, S], U32, name="xq_w", align_bytes=64)
        xq_s = sb.tile([P, S], U8, name="xq_s", align_bytes=64)
        xc_w = sb.tile([P, C], U32, name="xc_w", align_bytes=64)
        xc_s0 = sb.tile([P, C], U8, name="xc_s0", align_bytes=64)
        w_w = sb.tile([P, H], U32, name="w_w", align_bytes=64)
        w_s = sb.tile([P, H], U8, name="w_s", align_bytes=64)

        nc.vector.tensor_copy(xq_s[:], xs[:].indirect(offs_t[:]))
        nc.vector.tensor_copy(xq_w[:], xw[:].indirect(offs_t[:]))
        nc.vector.tensor_copy(dealt(w_w[:]), as_listed(ww[:]))
        nc.vector.tensor_copy(dealt(w_s[:]), as_listed(ws[:]))
        nc.vector.tensor_copy(xc_s0[:], xs[:].indirect(cand_t[:]))
        nc.vector.tensor_copy(dealt(xc_w[:]), xw[:].indirect(cand_t[:]))

        xc_s_first = sb.tile([P, P], U8, name="xc_s_first", align_bytes=64)
        nc.vector.tensor_copy(xc_s_first[:], as_listed(xc_s0[:])[:, :, 0])
        y_ps = [psum.tile([P, S], F32, name=f"y_ps{t}") for t in range(PACK)]
        s_ps = [psum.tile([P, S], F32, name=f"s_ps{t}") for t in range(PACK)]
        nst = [sb.tile([P, S], F32, name=f"nst{t}", align_bytes=64) for t in range(PACK)]
        z = sb.tile([P, PACK, S], F32, name="z", align_bytes=64)
        zi = sb.tile([P, S, PACK], BF16, name="zi", tag="zi", align_bytes=64)
        zq_w = [sb.tile([P, HALF], U32, name=f"zq_w{h}", align_bytes=64) for h in range(2)]
        zq_s = [sb.tile([P, HALF], U8, name=f"zq_s{h}", align_bytes=64) for h in range(2)]

        for t in range(PACK):
            cols = slice(t * P, (t + 1) * P)
            nc.tensor.matmul_mx(
                out=y_ps[t][:], lhsT=w_w[:, cols].bitcast(FP8X4), lhsT_scale=w_s[:, cols],
                rhs=xq_w[:].bitcast(FP8X4), rhs_scale=xq_s[:], start=True, stop=True,
            )
            nc.scalar.activation(win_a[t][:, :S], y_ps[t][:], COPY, scale=gs_t[:, t : t + 1])
            nc.scalar.activation(win_b[t][:, S:], y_ps[t][:], COPY, scale=gs_t[:, t : t + 1])
        for t in range(PACK):
            nc.vector.tensor_tensor(nst[t][:], win_a[t][:].indirect(n1_t[:]), win_b[t][:, S:], ALU.subtract)
            nc.scalar.activation(win_b[t][:, :S], nst[t][:], COPY, scale=0.5)

        halves = [slice(0, HALF), slice(HALF, S)]
        list_halves = [slice(0, HALF // 16), slice(HALF // 16, S // 16)]

        def weave(dst, src, rows, cols, on_scalar):
            out_ap = dst[:, cols, rows]
            in_ap = src[:, rows, cols].rearrange("p t n -> p n t")
            if on_scalar:
                nc.scalar.copy(out_ap, in_ap)
            else:
                nc.vector.tensor_copy(out_ap, in_ap)

        def quantise(words, scales, src, cols):
            nc.vector.quantize_mx(
                out=words.bitcast(FP8X4), scales=scales,
                in_=src[:, cols, :].rearrange("p n t -> p (n t)"),
            )

        whole = slice(0, S)
        last = PACK - 1
        for t in range(last):
            nc.vector.tensor_tensor(z[:, t, :], win_b[t][:].indirect(n1_t[:]), nst[t][:], ALU.subtract)
            if t == 1:
                weave(zi, z, slice(0, 2), whole, True)
        for h in range(2):
            nc.vector.tensor_tensor(
                z[:, last, halves[h]], win_b[last][:].indirect(n1_t[:, list_halves[h]]), nst[last][:, halves[h]], ALU.subtract
            )
            weave(zi, z, slice(2, 4), halves[h], h == 0)
        for h in (1, 0):
            quantise(zq_w[h][:], zq_s[h][:], zi, halves[h])
        xc_s_rest = sb.tile([P, last * P], U8, name="xc_s_rest", tag="zi", align_bytes=64)
        nc.vector.tensor_copy(xc_s_rest[:].rearrange("p (t m) -> p m t", t=last), as_listed(xc_s0[:])[:, :, 1:])
        xc_s = [xc_s_first[:]] + [xc_s_rest[:, t * P : (t + 1) * P] for t in range(last)]

        neg_s = [sb.tile([P, S], F32, name=f"neg_s{t}", align_bytes=64) for t in range(PACK)]

        def scores(t, bank, h):
            nc.tensor.matmul_mx(
                out=bank[:, halves[h]], lhsT=xc_w[:, t * P : (t + 1) * P].bitcast(FP8X4), lhsT_scale=xc_s[t],
                rhs=zq_w[h][:].bitcast(FP8X4), rhs_scale=zq_s[h][:], start=True, stop=True,
            )

        for h, bank in ((1, y_ps[0]), (0, s_ps[0])):
            scores(0, bank, h)
            nc.scalar.activation(win_a[0][:, halves[h]], bank[:, halves[h]], COPY, scale=0.0625)
        nc.vector.tensor_scalar(neg_s[0][:, halves[1]], y_ps[0][:, halves[1]], -0.0625, None, ALU.mult)
        nc.scalar.activation(neg_s[0][:, halves[0]], s_ps[0][:, halves[0]], COPY, scale=-0.0625)
        for t in range(1, PACK):
            for h in range(2):
                scores(t, s_ps[t], h)
            nc.scalar.activation(win_a[t][:, :S], s_ps[t][:], COPY, scale=0.0625)
            nc.scalar.activation(neg_s[t][:], s_ps[t][:], COPY, scale=-0.0625)

        res = sb.tile([P, PACK, S], F32, name="res", align_bytes=64)
        ri = sb.tile([P, S, PACK], BF16, name="ri", align_bytes=64)
        rq_w = sb.tile([P, S], U32, name="rq_w", align_bytes=64)
        rq_s = sb.tile([P, S], U8, name="rq_s", align_bytes=64)
        da = [sb.tile([P, S], F32, name=f"da{t}", align_bytes=64) for t in range(PACK)]
        db = [sb.tile([P, S], F32, name=f"db{t}", align_bytes=64) for t in range(PACK)]
        up = [sb.tile([P, S], F32, name=f"up{t}", align_bytes=64) for t in range(PACK)]
        below = sb.tile([P, S], F32, name="below", align_bytes=64)
        low_t = sb.tile([P, S], F32, name="low_t", align_bytes=64)
        rise_t = sb.tile([P, S], F32, name="rise_t", align_bytes=64)
        sum_t = sb.tile([P, S], F32, name="sum_t", align_bytes=64)
        out_rows = out_0.rearrange("(p t) n -> p t n", t=PACK)

        def turned_sum(bank, terms):
            for b in range(S // P):
                blk = slice(b * P, (b + 1) * P)
                for i, term in enumerate(terms):
                    nc.tensor.matmul(
                        bank[:, blk], term[:, blk], ident[:], start=i == 0, stop=i == len(terms) - 1, is_transpose=True
                    )

        def fetch(dst, t, lst, cols, list_cols):
            nc.vector.tensor_tensor(dst[t][:, cols], win_a[t][:].indirect(lst[:, list_cols]), neg_s[t][:, cols], ALU.add)

        def cap(t, cols):
            nc.vector.scalar_tensor_tensor(up[t][:, cols], da[t][:, cols], 0.0, db[t][:, cols], ALU.max, ALU.min)

        def floor(t, cols):
            nc.vector.scalar_tensor_tensor(db[t][:, cols], da[t][:, cols], 0.0, up[t][:, cols], ALU.min, ALU.max)

        def finish(t, cols):
            nc.vector.tensor_tensor(res[:, t, cols], db[t][:, cols], neg_s[t][:, cols], ALU.subtract)
            nc.sync.dma_start(out_rows[:, t, cols], res[:, t, cols])

        def store_from(bank, t):
            nc.scalar.copy(res[:, t, :], bank[:])
            nc.sync.dma_start(out_rows[:, t, :], res[:, t, :])

        all16 = slice(0, S // 16)
        for h in (1, 0):
            fetch(da, 0, n2_t, halves[h], list_halves[h])
        nc.scalar.activation(below[:], da[0][:], RELU, scale=-1.0)
        turned_sum(y_ps[1], [below, neg_s[0]])
        nc.scalar.activation(low_t[:], y_ps[1][:], COPY, scale=-1.0)
        fetch(db, 0, n3_t, whole, all16)
        fetch(da, 1, n2_t, whole, all16)
        cap(0, whole)
        turned_sum(y_ps[2], [up[0], below])
        nc.scalar.activation(rise_t[:], y_ps[2][:], RELU)
        turned_sum(s_ps[0], [low_t, rise_t])
        store_from(s_ps[0], 0)
        weave(ri, res, slice(0, 1), halves[0], True)
        fetch(db, 1, n3_t, whole, all16)
        fetch(da, 2, n2_t, halves[0], list_halves[0])
        cap(1, whole)
        fetch(da, 2, n2_t, halves[1], list_halves[1])
        floor(1, whole)
        turned_sum(y_ps[3], [win_a[1], db[1]])
        nc.scalar.copy(sum_t[:], y_ps[3][:])
        turned_sum(s_ps[1], [sum_t])
        store_from(s_ps[1], 1)
        weave(ri, res, slice(0, 2), halves[1], True)
        fetch(db, 2, n3_t, whole, all16)
        fetch(da, 3, n2_t, whole, all16)
        cap(2, whole)
        fetch(db, 3, n3_t, whole, all16)
        floor(2, whole)
        cap(3, halves[0])
        finish(2, whole)
        cap(3, halves[1])
        floor(3, halves[0])
        floor(3, halves[1])
        words_out = out_1[0].rearrange("p n t -> p (n t)").bitcast(I32)
        finish(3, halves[0])
        weave(ri, res, slice(1, 4), halves[0], True)
        finish(3, halves[1])
        weave(ri, res, slice(2, 4), halves[1], False)
        for h in range(2):
            quantise(rq_w[:, halves[h]], rq_s[:, halves[h]], ri, halves[h])
            nc.sync.dma_start(words_out[:, halves[h]], rq_w[:, halves[h]].bitcast(I32))
        for q in range(4):
            queue = nc.scalar if q < 2 else nc.sync
            queue.dma_start(out_2[0, 4 * q : 4 * q + 4, :].bitcast(I32), rq_s[32 * q : 32 * q + 4, :].bitcast(I32))
